import numpy as np
import ml_dtypes


def mxq(x, axis, fmt="e4m3"):
    dtype, down = {"e4m3": (ml_dtypes.float8_e4m3fn, 7), "e5m2": (ml_dtypes.float8_e5m2, 14)}[fmt]
    v = np.moveaxis(np.asarray(x, np.float32).astype(ml_dtypes.bfloat16).astype(np.float64), axis, -1)
    blocks = v.reshape(v.shape[:-1] + (-1, 32))
    amax = np.abs(blocks).max(-1, keepdims=True)
    byte = np.maximum(np.where(amax > 0, np.frexp(amax)[1] - 1 + 127, 0) - down, 1)
    scale = np.exp2(byte - 127.0)
    codes = (blocks / scale).astype(np.float32).astype(dtype).astype(np.float64)
    return np.moveaxis((codes * scale).reshape(v.shape), -1, axis)


WIDE = False


def mx_kscale(k):
    if not WIDE:
        return np.ones(k)
    levels = np.array([10, -10, 5, -5, 0])
    if k % 512:
        return np.exp2(np.random.permutation(np.resize(levels, k // 32))).repeat(32)
    a = np.empty((k // 512, 16))
    for p in range(k // 512):
        a[p, :8] = np.random.permutation(np.resize(levels, 8))
        for g in range(8):
            far = levels[np.abs(levels - a[p, g]) >= 10]
            a[p, g + 8] = far[np.random.randint(len(far))]
    return np.exp2(a.ravel()).repeat(32)


def f64(x):
    return np.asarray(x).astype(np.float64)


def striped(idx):
    return np.tile(idx.reshape(-1, 16).T, (8, 1)).astype(np.uint16)


def unstriped(offs):
    return offs[:16].T.reshape(-1).astype(np.int64)


E2M1 = np.array([0.0, 0.5, 1.0, 1.5, 2.0, 3.0, 4.0, 6.0, -0.0, -0.5, -1.0, -1.5, -2.0, -3.0, -4.0, -6.0])


def pack_weight(w, fmt):
    k, n = w.shape
    w = f64(np.asarray(w, np.float32).astype(ml_dtypes.bfloat16)).reshape(k // 32, 32, n)
    amax = np.abs(w).max(1)
    if fmt == "e4m3":
        byte = np.frexp(amax)[1] - 1 + 127 - 7
    else:
        mant, ex = np.frexp(amax / 6.0)
        byte = np.where(mant > 0.5, ex, ex - 1) + 127
    byte = np.clip(np.where(amax > 0, byte, 1), 1, 254)
    scaled = (w * np.exp2(127.0 - byte)[:, None, :]).reshape(k, n).astype(np.float32)
    by_word = np.ascontiguousarray(scaled.reshape(k // 512, 128, 4, n).transpose(0, 1, 3, 2))
    if fmt == "e4m3":
        words = by_word.astype(ml_dtypes.float8_e4m3fn).view(np.uint8)
    else:
        c = by_word.astype(ml_dtypes.float4_e2m1fn).view(np.uint8) & 0xF
        words = (c[..., 0::2] | (c[..., 1::2] << 4)).reshape(k // 512, 128, 2 * n)
    return np.ascontiguousarray(words), np.ascontiguousarray(byte.astype(np.uint8).reshape(k // 512, 16, n))


def unpack_weight(words, scales, fmt):
    g, _, n = scales.shape
    words = np.ascontiguousarray(words).reshape(g, 128, n, -1)
    if fmt == "e4m3":
        vals = words.view(ml_dtypes.float8_e4m3fn).astype(np.float64)
    else:
        nib = np.empty((g, 128, n, 4), np.uint8)
        nib[..., 0::2] = words & 0xF
        nib[..., 1::2] = words >> 4
        vals = E2M1[nib]
    vals = vals * np.repeat(np.exp2(scales.astype(np.float64) - 127.0), 8, axis=1)[..., None]
    return vals.transpose(0, 1, 3, 2).reshape(g * 512, n)


def sigmoid(v):
    return 1.0 / (1.0 + np.exp(-np.maximum(v, -700.0)))


K, T, E, C, H, N = 2048, 768, 2, 256, 512, 384


def by_expert(wq, xq):
    return np.concatenate([wq[e].T @ xq[:, e * C:(e + 1) * C] for e in range(E)], axis=1)


def setup_inputs():
    n = np.random.standard_normal
    s = mx_kscale(K)[:, None]
    u = mx_kscale(H)
    w1 = [pack_weight(m, "e2m1") for m in n((E, K, H)) / np.sqrt(K) / s[None]]
    w3 = [pack_weight(m, "e2m1") for m in n((E, K, H)) / np.sqrt(K) / s[None] * u[None, None, :]]
    w2 = [pack_weight(m, "e2m1") for m in n((E, H, N)) / np.sqrt(H) / u[None, :, None]]
    x = pack_weight(n((K, T)) * s, "e4m3")
    return {
        "x_words": x[0],
        "x_scales": x[1],
        "xr": n((N, T)).astype(np.float32),
        "w1_words": np.stack([m[0] for m in w1]),
        "w1_scales": np.stack([m[1] for m in w1]),
        "w3_words": np.stack([m[0] for m in w3]),
        "w3_scales": np.stack([m[1] for m in w3]),
        "w2_words": np.stack([m[0] for m in w2]),
        "w2_scales": np.stack([m[1] for m in w2]),
        "gate": np.tile(np.random.uniform(0.2, 1.0, E * C), (N, 1)).astype(np.float32),
        "offs": striped(np.random.permutation(T)[:E * C]),
    }


def reference(x_words, x_scales, xr, w1_words, w1_scales, w3_words, w3_scales, w2_words, w2_scales, gate, offs):
    idx = unstriped(offs)
    w1 = np.stack([unpack_weight(w1_words[e], w1_scales[e], "e2m1") for e in range(E)])
    w3 = np.stack([unpack_weight(w3_words[e], w3_scales[e], "e2m1") for e in range(E)])
    w2 = np.stack([unpack_weight(w2_words[e], w2_scales[e], "e2m1") for e in range(E)])
    xq = unpack_weight(x_words, x_scales, "e4m3")[:, idx]
    h = sigmoid(by_expert(w1, xq))
    h = h * by_expert(w3, xq)
    y = by_expert(w2, mxq(h, 0, "e4m3"))
    out = f64(xr).copy()
    out[:, idx] += f64(gate) * y
    return out

@@ -1,0 +1,190 @@
+from contextlib import ExitStack
+
+import concourse.mybir as mybir
+from concourse.masks import make_identity
+
+K, T, E, C, H, N = 2048, 768, 2, 256, 512, 384
+FLOPS = 2 * E * C * (2 * K * H + H * N)
+
+F32 = mybir.dt.float32
+BF16 = mybir.dt.bfloat16
+I32 = mybir.dt.int32
+U32 = mybir.dt.uint32
+U16 = mybir.dt.uint16
+U8 = mybir.dt.uint8
+FP8X4 = mybir.dt.float8_e4m3fn_x4
+FP4X4 = mybir.dt.float4_e2m1fn_x4
+MULT = mybir.AluOpType.mult
+ADD = mybir.AluOpType.add
+SIGMOID = mybir.ActivationFunctionType.Sigmoid
+
+P = 128
+PASSES = K // 512
+TILES = C // P
+BLOCKS = N // P
+LIST_COLS = C // 16
+
+
+def tile_moe_res_glu_sigmoid_kernel(
+    tc, x_words, x_scales, xr, w1_words, w1_scales, w3_words, w3_scales, w2_words, w2_scales, gate, offs, out
+):
+    nc = tc.nc
+    with ExitStack() as ctx:
+        keep = ctx.enter_context(tc.tile_pool(name="keep", bufs=1))
+        psum = ctx.enter_context(tc.psum_pool(name="psum", bufs=1))
+
+        def sbuf(shape, dtype, name):
+            return keep.tile(shape, dtype, name=name, align_bytes=64)
+
+        offsets = keep.tile([P, E * LIST_COLS], U16, name="offsets")
+        x_table = [sbuf([P, T], U32, f"x_table{s}") for s in range(PASSES)]
+        x_plane = sbuf([P, PASSES, T], U8, "x_plane")
+        first_words = [[sbuf([P, PASSES, 2 * H], U8, f"words{m}_{e}") for m in range(2)] for e in range(E)]
+        first_plane = [[sbuf([P, PASSES, H], U8, f"plane{m}_{e}") for m in range(2)] for e in range(E)]
+        w2_sb = sbuf([P, E, 2 * N], U8, "w2_sb")
+        w2_plane = sbuf([P, E, N], U8, "w2_plane")
+        gate_sb = sbuf([P, E * C], F32, "gate_sb")
+        resid = sbuf([P, BLOCKS, T], F32, "resid")
+        spread = [sbuf([P, T], F32, f"spread{b}") for b in range(BLOCKS)]
+        identity = sbuf([P, P], F32, "identity")
+        banks = [psum.tile([P, 512], F32, name=f"bank{j}") for j in range(8)]
+
+        def zero_plane(plane):
+            nc.vector.memset(plane[:].rearrange("p a n -> p (a n)").bitcast(I32), 0)
+
+        def load_plane(plane, rows):
+            view = rows.bitcast(I32).rearrange("a (q r) n -> r q a n", r=4)
+            for r in range(4):
+                nc.sync.dma_start(out=plane[r:P:32, :, :].bitcast(I32), in_=view[r])
+
+        def load_x(s):
+            nc.sync.dma_start(out=x_table[s][:].bitcast(I32), in_=x_words[s].rearrange("p t r -> p (t r)").bitcast(I32))
+
+        def load_first(e, m):
+            load_plane(first_plane[e][m], (w1_scales, w3_scales)[m][e])
+            words = (w1_words, w3_words)[m][e]
+            nc.sync.dma_start(out=first_words[e][m][:].bitcast(I32), in_=words.bitcast(I32).rearrange("s p n -> p s n"))
+
+        zero_plane(x_plane)
+        for m in range(2):
+            zero_plane(first_plane[0][m])
+        zero_plane(w2_plane)
+        for m in range(2):
+            zero_plane(first_plane[1][m])
+        nc.vector.memset(spread[0][:], 0.0)
+        for b in range(1, BLOCKS):
+            nc.scalar.copy(out=spread[b][:], in_=spread[0][:])
+        make_identity(nc, identity[:])
+
+        nc.sync.dma_start(offsets[:], offs)
+        load_x(0)
+        load_plane(x_plane, x_scales)
+        load_x(1)
+        load_first(0, 0)
+        load_x(2)
+        load_x(3)
+        load_first(0, 1)
+        nc.sync.dma_start(out=w2_sb[:].bitcast(I32), in_=w2_words.bitcast(I32).rearrange("e s p n -> p (e s) n"))
+        load_plane(w2_plane, w2_scales.rearrange("e s q n -> (e s) q n"))
+        nc.sync.dma_start(out=gate_sb[:], in_=gate[0:P, :])
+        load_first(1, 0)
+        load_first(1, 1)
+        nc.sync.dma_start(out=resid[:], in_=xr.rearrange("(b p) t -> p b t", p=P))
+
+        def slots(first, count):
+            return offsets[:, first // 16 : (first + count) // 16]
+
+        def acc(e, j, m):
+            return banks[4 * e + 2 * j + m]
+
+        slot_words = [[sbuf([P, C], U32, f"slot_words{e}_{s}") for s in range(PASSES)] for e in range(E)]
+        slot_plane = [[sbuf([P, C], U8, f"slot_plane{e}_{s}") for s in range(PASSES)] for e in range(E)]
+
+        def gather(e):
+            for s in range(PASSES):
+                nc.vector.tensor_copy(slot_words[e][s][:], x_table[s][:].indirect(slots(e * C, C)))
+                nc.vector.tensor_copy(slot_plane[e][s][:], x_plane[:, s, :].indirect(slots(e * C, C)))
+
+        def first(e, j):
+            cols = slice(j * P, (j + 1) * P)
+            for m in range(2):
+                for s in range(PASSES):
+                    nc.tensor.matmul_mx(
+                        out=acc(e, j, m)[:],
+                        lhsT=slot_words[e][s][:, cols].bitcast(FP8X4),
+                        lhsT_scale=slot_plane[e][s][:, cols],
+                        rhs=first_words[e][m][:, s, :].bitcast(FP4X4),
+                        rhs_scale=first_plane[e][m][:, s, :],
+                        start=(s == 0),
+                        stop=(s == PASSES - 1),
+                    )
+
+        h_turned = [[sbuf([P, P * 4], BF16, f"h_turned{e}_{j}") for j in range(TILES)] for e in range(E)]
+
+        def hidden(e, j):
+            order = "c (p u d) -> c u p d"
+            sig = sbuf([P, 2, P, 2], F32, f"sig{e}_{j}")
+            h = sbuf([P, 2, P, 2], BF16, f"h{e}_{j}")
+            nc.scalar.activation(out=sig[:], in_=acc(e, j, 0)[:].rearrange(order, u=2, d=2), func=SIGMOID)
+            nc.vector.tensor_tensor(out=h[:], in0=acc(e, j, 1)[:].rearrange(order, u=2, d=2), in1=sig[:], op=MULT)
+            pairs = h[:].rearrange("c u p d -> c (u p d)").bitcast(F32)
+            turned = acc(e, j, 0)
+            for u in range(2):
+                nc.tensor.transpose(turned[:, u * P : (u + 1) * P], pairs[:, u * P : (u + 1) * P], identity[:])
+            nc.scalar.copy(
+                out=h_turned[e][j][:].bitcast(F32).rearrange("p (c u) -> p c u", u=2),
+                in_=turned[:, 0 : 2 * P].rearrange("p (u c) -> p c u", u=2),
+            )
+
+        y = [[sbuf([P, BLOCKS, P], F32, f"y{e}_{j}") for j in range(TILES)] for e in range(E)]
+
+        def second(e, j):
+            codes = sbuf([P, P], U32, f"h_codes{e}_{j}")
+            plane = sbuf([P, P], U8, f"h_plane{e}_{j}")
+            nc.vector.quantize_mx(out=codes[:].bitcast(FP8X4), scales=plane[:], in_=h_turned[e][j][:])
+            bank = acc(e, j, 1)
+            for b in range(BLOCKS):
+                nc.tensor.matmul_mx(
+                    out=bank[:, b * P : (b + 1) * P],
+                    lhsT=w2_sb[:, e, 2 * b * P : 2 * (b + 1) * P].bitcast(FP4X4),
+                    lhsT_scale=w2_plane[:, e, b * P : (b + 1) * P],
+                    rhs=codes[:].bitcast(FP8X4),
+                    rhs_scale=plane[:],
+                    start=True,
+                    stop=True,
+                )
+            nc.scalar.copy(out=y[e][j][:].rearrange("p b c -> p (b c)"), in_=bank[:, 0:N])
+
+        def scatter(e, j, b):
+            first_slot = e * C + j * P
+            nc.vector.tensor_tensor(
+                spread[b][:].indirect(slots(first_slot, P)), y[e][j][:, b, :], gate_sb[:, first_slot : first_slot + P], MULT
+            )
+
+        def finish(b):
+            nc.vector.tensor_tensor(out=resid[:, b, :], in0=resid[:, b, :], in1=spread[b][:], op=ADD)
+            nc.sync.dma_start(out=out[b * P : (b + 1) * P, :], in_=resid[:, b, :])
+
+        gather(0)
+        first(0, 0)
+        first(0, 1)
+        gather(1)
+        hidden(0, 0)
+        hidden(0, 1)
+        second(0, 0)
+        second(0, 1)
+        first(1, 0)
+        first(1, 1)
+        hidden(1, 0)
+        hidden(1, 1)
+        second(1, 0)
+        second(1, 1)
+        for e, j in ((0, 0), (0, 1), (1, 0)):
+            for b in range(BLOCKS):
+                scatter(e, j, b)
+        scatter(1, 1, 0)
+        scatter(1, 1, 1)
+        finish(0)
+        scatter(1, 1, 2)
+        finish(1)
+        finish(2)

@@ -19,10 +19,19 @@ ADD = mybir.AluOpType.add
 SIGMOID = mybir.ActivationFunctionType.Sigmoid
 
 P = 128
-PASSES = K // 512
+PASSES = K // (4 * P)
+HALF = PASSES // 2
 TILES = C // P
 BLOCKS = N // P
-LIST_COLS = C // 16
+PER_COLUMN = 16
+ROWS = 4
+BANK = 512
+LAST_PARTS = 3
+
+AT_SIGMOID = 0
+AT_TURNED = AT_SIGMOID + 4 * H
+AT_TABLE = AT_TURNED + 2 * H
+AT_WINDOW = AT_TABLE + 4 * T
 
 
 def tile_moe_res_glu_sigmoid_kernel(
@@ -31,160 +40,216 @@ def tile_moe_res_glu_sigmoid_kernel(
     nc = tc.nc
     with ExitStack() as ctx:
         keep = ctx.enter_context(tc.tile_pool(name="keep", bufs=1))
+        turns = ctx.enter_context(tc.tile_pool(name="turns", bufs=1))
         psum = ctx.enter_context(tc.psum_pool(name="psum", bufs=1))
 
-        def sbuf(shape, dtype, name):
-            return keep.tile(shape, dtype, name=name, align_bytes=64)
+        def sbuf(shape, dtype, name, at=None):
+            if at is None:
+                return keep.tile(shape, dtype, name=name, align_bytes=64)
+            return turns.tile(shape, dtype, name=name, align_bytes=64, offset=at)
 
-        offsets = keep.tile([P, E * LIST_COLS], U16, name="offsets")
-        x_table = [sbuf([P, T], U32, f"x_table{s}") for s in range(PASSES)]
+        tiles = [(e, j) for e in range(E) for j in range(TILES)]
+        last_pass, last_block = PASSES - 1, BLOCKS - 1
+
+        offsets = keep.tile([P, E * C // PER_COLUMN], U16, name="offsets")
+        x_table = [sbuf([P, T], U32, f"x_table{s}", AT_TABLE if s == last_pass else None) for s in range(PASSES)]
         x_plane = sbuf([P, PASSES, T], U8, "x_plane")
-        first_words = [[sbuf([P, PASSES, 2 * H], U8, f"words{m}_{e}") for m in range(2)] for e in range(E)]
-        first_plane = [[sbuf([P, PASSES, H], U8, f"plane{m}_{e}") for m in range(2)] for e in range(E)]
+        w_words = {
+            (e, m, half): sbuf([P, HALF, 2 * H], U8, f"w_words{e}{m}{half}") for e in range(E) for m in range(2) for half in range(2)
+        }
+        w_plane = {(e, m): sbuf([P, PASSES, H], U8, f"w_plane{e}{m}") for e in range(E) for m in range(2)}
         w2_sb = sbuf([P, E, 2 * N], U8, "w2_sb")
         w2_plane = sbuf([P, E, N], U8, "w2_plane")
         gate_sb = sbuf([P, E * C], F32, "gate_sb")
         resid = sbuf([P, BLOCKS, T], F32, "resid")
-        spread = [sbuf([P, T], F32, f"spread{b}") for b in range(BLOCKS)]
+        window = [sbuf([P, T], F32, f"window{b}", AT_WINDOW if b == 0 else None) for b in range(BLOCKS)]
         identity = sbuf([P, P], F32, "identity")
-        banks = [psum.tile([P, 512], F32, name=f"bank{j}") for j in range(8)]
+        banks = [psum.tile([P, BANK], F32, name=f"bank{n}") for n in range(2 * len(tiles))]
 
-        def zero_plane(plane):
+        slot_words = {
+            (e, s): sbuf([P, C], U32, f"slot_words{e}{s}", AT_SIGMOID if (e, s) == (1, 2) else None)
+            for e in range(E)
+            for s in range(PASSES)
+        }
+        slot_plane = {(0, s): sbuf([P, C], U8, f"slot_plane0{s}") for s in range(PASSES)}
+        for s in range(PASSES):
+            slot_plane[1, s] = sbuf([P, C], U8, f"slot_plane1{s}", AT_TURNED if s == last_pass else AT_TABLE + s * C)
+        sigmoid = {(e, j): sbuf([P, 2, P, 2], F32, f"sigmoid{e}{j}", AT_SIGMOID if (e, j) == (0, 1) else None) for e, j in tiles}
+        h = {(e, j): sbuf([P, 2, P, 2], BF16, f"h{e}{j}") for e, j in tiles}
+        h_turned = {(e, j): sbuf([P, 4 * P], BF16, f"h_turned{e}{j}", AT_TURNED if (e, j) == (0, 0) else None) for e, j in tiles}
+        h_words = {(e, j): sbuf([P, P], U32, f"h_words{e}{j}") for e, j in tiles}
+        h_plane = {(e, j): sbuf([P, P], U8, f"h_plane{e}{j}") for e, j in tiles}
+        y = {
+            (e, j, b): sbuf([P, P], F32, f"y{e}{j}{b}", AT_WINDOW if (e, j, b) == (1, 1, last_block) else None)
+            for e, j in tiles
+            for b in range(BLOCKS)
+        }
+
+        for plane in (x_plane, w_plane[0, 0], w_plane[0, 1], w2_plane, w_plane[1, 0], w_plane[1, 1]):
             nc.vector.memset(plane[:].rearrange("p a n -> p (a n)").bitcast(I32), 0)
+        make_identity(nc, identity[:])
+        for b in range(BLOCKS):
+            nc.vector.memset(window[b][:], 0.0)
 
-        def load_plane(plane, rows):
-            view = rows.bitcast(I32).rearrange("a (q r) n -> r q a n", r=4)
-            for r in range(4):
-                nc.sync.dma_start(out=plane[r:P:32, :, :].bitcast(I32), in_=view[r])
+        def load_plane(plane, scales):
+            rows = scales.bitcast(I32).rearrange("a (q r) n -> r q a n", r=ROWS)
+            for r in range(ROWS):
+                nc.sync.dma_start(out=plane[r:P:32, :, :].bitcast(I32), in_=rows[r])
 
         def load_x(s):
             nc.sync.dma_start(out=x_table[s][:].bitcast(I32), in_=x_words[s].rearrange("p t r -> p (t r)").bitcast(I32))
 
-        def load_first(e, m):
-            load_plane(first_plane[e][m], (w1_scales, w3_scales)[m][e])
-            words = (w1_words, w3_words)[m][e]
-            nc.sync.dma_start(out=first_words[e][m][:].bitcast(I32), in_=words.bitcast(I32).rearrange("s p n -> p s n"))
+        def load_w_plane(e, m):
+            load_plane(w_plane[e, m], (w1_scales, w3_scales)[m][e])
 
-        zero_plane(x_plane)
-        for m in range(2):
-            zero_plane(first_plane[0][m])
-        zero_plane(w2_plane)
-        for m in range(2):
-            zero_plane(first_plane[1][m])
-        nc.vector.memset(spread[0][:], 0.0)
-        for b in range(1, BLOCKS):
-            nc.scalar.copy(out=spread[b][:], in_=spread[0][:])
-        make_identity(nc, identity[:])
+        def load_w_words(e, m, half):
+            words = (w1_words, w3_words)[m][e, half * HALF : (half + 1) * HALF]
+            nc.sync.dma_start(out=w_words[e, m, half][:].bitcast(I32), in_=words.bitcast(I32).rearrange("s p n -> p s n"))
 
         nc.sync.dma_start(offsets[:], offs)
         load_x(0)
         load_plane(x_plane, x_scales)
         load_x(1)
-        load_first(0, 0)
+        for m in range(2):
+            load_w_plane(0, m)
+            load_w_words(0, m, 0)
         load_x(2)
         load_x(3)
-        load_first(0, 1)
+        for m in range(2):
+            load_w_words(0, m, 1)
+        load_w_plane(1, 0)
+        load_w_words(1, 0, 0)
         nc.sync.dma_start(out=w2_sb[:].bitcast(I32), in_=w2_words.bitcast(I32).rearrange("e s p n -> p (e s) n"))
         load_plane(w2_plane, w2_scales.rearrange("e s q n -> (e s) q n"))
+        load_w_plane(1, 1)
+        load_w_words(1, 1, 0)
         nc.sync.dma_start(out=gate_sb[:], in_=gate[0:P, :])
-        load_first(1, 0)
-        load_first(1, 1)
+        for m in range(2):
+            load_w_words(1, m, 1)
         nc.sync.dma_start(out=resid[:], in_=xr.rearrange("(b p) t -> p b t", p=P))
 
         def slots(first, count):
-            return offsets[:, first // 16 : (first + count) // 16]
+            return offsets[:, first // PER_COLUMN : (first + count) // PER_COLUMN]
 
-        def acc(e, j, m):
-            return banks[4 * e + 2 * j + m]
+        def sum_bank(e, j, m):
+            return banks[2 * (TILES * e + j) + m]
 
-        slot_words = [[sbuf([P, C], U32, f"slot_words{e}_{s}") for s in range(PASSES)] for e in range(E)]
-        slot_plane = [[sbuf([P, C], U8, f"slot_plane{e}_{s}") for s in range(PASSES)] for e in range(E)]
+        def y_bank(e, j, b):
+            return sum_bank(1, 0, 1) if (e, j) == (0, 1) and b > 0 else sum_bank(0, j, 1)
 
-        def gather(e):
-            for s in range(PASSES):
-                nc.vector.tensor_copy(slot_words[e][s][:], x_table[s][:].indirect(slots(e * C, C)))
-                nc.vector.tensor_copy(slot_plane[e][s][:], x_plane[:, s, :].indirect(slots(e * C, C)))
+        def gather_words(e, s):
+            nc.vector.tensor_copy(slot_words[e, s][:], x_table[s][:].indirect(slots(e * C, C)))
 
-        def first(e, j):
+        def gather_plane(e, s):
+            nc.vector.tensor_copy(slot_plane[e, s][:], x_plane[:, s, :].indirect(slots(e * C, C)))
+
+        def first_pass(e, j, m, s):
             cols = slice(j * P, (j + 1) * P)
-            for m in range(2):
-                for s in range(PASSES):
-                    nc.tensor.matmul_mx(
-                        out=acc(e, j, m)[:],
-                        lhsT=slot_words[e][s][:, cols].bitcast(FP8X4),
-                        lhsT_scale=slot_plane[e][s][:, cols],
-                        rhs=first_words[e][m][:, s, :].bitcast(FP4X4),
-                        rhs_scale=first_plane[e][m][:, s, :],
-                        start=(s == 0),
-                        stop=(s == PASSES - 1),
-                    )
+            nc.tensor.matmul_mx(
+                out=sum_bank(e, j, m)[:],
+                lhsT=slot_words[e, s][:, cols].bitcast(FP8X4),
+                lhsT_scale=slot_plane[e, s][:, cols],
+                rhs=w_words[e, m, s // HALF][:, s % HALF, :].bitcast(FP4X4),
+                rhs_scale=w_plane[e, m][:, s, :],
+                start=(s == 0),
+                stop=(s == last_pass),
+            )
 
-        h_turned = [[sbuf([P, P * 4], BF16, f"h_turned{e}_{j}") for j in range(TILES)] for e in range(E)]
+        def first_layer(e):
+            for m in range(2):
+                for s in range(HALF):
+                    for j in range(TILES):
+                        first_pass(e, j, m, s)
+            for j in range(TILES):
+                for m in range(2):
+                    for s in range(HALF, PASSES):
+                        first_pass(e, j, m, s)
 
         def hidden(e, j):
             order = "c (p u d) -> c u p d"
-            sig = sbuf([P, 2, P, 2], F32, f"sig{e}_{j}")
-            h = sbuf([P, 2, P, 2], BF16, f"h{e}_{j}")
-            nc.scalar.activation(out=sig[:], in_=acc(e, j, 0)[:].rearrange(order, u=2, d=2), func=SIGMOID)
-            nc.vector.tensor_tensor(out=h[:], in0=acc(e, j, 1)[:].rearrange(order, u=2, d=2), in1=sig[:], op=MULT)
-            pairs = h[:].rearrange("c u p d -> c (u p d)").bitcast(F32)
-            turned = acc(e, j, 0)
+            nc.scalar.activation(out=sigmoid[e, j][:], in_=sum_bank(e, j, 0)[:].rearrange(order, u=2, d=2), func=SIGMOID)
+            nc.vector.tensor_tensor(
+                out=h[e, j][:], in0=sum_bank(e, j, 1)[:].rearrange(order, u=2, d=2), in1=sigmoid[e, j][:], op=MULT
+            )
+            pairs = h[e, j][:].rearrange("c u p d -> c (u p d)").bitcast(F32)
+            turned = sum_bank(e, j, 0)
             for u in range(2):
                 nc.tensor.transpose(turned[:, u * P : (u + 1) * P], pairs[:, u * P : (u + 1) * P], identity[:])
             nc.scalar.copy(
-                out=h_turned[e][j][:].bitcast(F32).rearrange("p (c u) -> p c u", u=2),
+                out=h_turned[e, j][:].bitcast(F32).rearrange("p (c u) -> p c u", u=2),
                 in_=turned[:, 0 : 2 * P].rearrange("p (u c) -> p c u", u=2),
             )
 
-        y = [[sbuf([P, BLOCKS, P], F32, f"y{e}_{j}") for j in range(TILES)] for e in range(E)]
+        def quantise(e, j):
+            nc.vector.quantize_mx(out=h_words[e, j][:].bitcast(FP8X4), scales=h_plane[e, j][:], in_=h_turned[e, j][:])
 
-        def second(e, j):
-            codes = sbuf([P, P], U32, f"h_codes{e}_{j}")
-            plane = sbuf([P, P], U8, f"h_plane{e}_{j}")
-            nc.vector.quantize_mx(out=codes[:].bitcast(FP8X4), scales=plane[:], in_=h_turned[e][j][:])
-            bank = acc(e, j, 1)
-            for b in range(BLOCKS):
+        def second_layer(e, j, blocks):
+            for b in blocks:
                 nc.tensor.matmul_mx(
-                    out=bank[:, b * P : (b + 1) * P],
+                    out=y_bank(e, j, b)[:, b * P : (b + 1) * P],
                     lhsT=w2_sb[:, e, 2 * b * P : 2 * (b + 1) * P].bitcast(FP4X4),
                     lhsT_scale=w2_plane[:, e, b * P : (b + 1) * P],
-                    rhs=codes[:].bitcast(FP8X4),
-                    rhs_scale=plane[:],
+                    rhs=h_words[e, j][:].bitcast(FP8X4),
+                    rhs_scale=h_plane[e, j][:],
                     start=True,
                     stop=True,
                 )
-            nc.scalar.copy(out=y[e][j][:].rearrange("p b c -> p (b c)"), in_=bank[:, 0:N])
+
+        def leave_psum(e, j, blocks):
+            for b in blocks:
+                nc.scalar.copy(out=y[e, j, b][:], in_=y_bank(e, j, b)[:, b * P : (b + 1) * P])
 
         def scatter(e, j, b):
-            first_slot = e * C + j * P
-            nc.vector.tensor_tensor(
-                spread[b][:].indirect(slots(first_slot, P)), y[e][j][:, b, :], gate_sb[:, first_slot : first_slot + P], MULT
-            )
+            first = e * C + j * P
+            nc.vector.tensor_tensor(window[b][:].indirect(slots(first, P)), y[e, j, b][:], gate_sb[:, first : first + P], MULT)
 
-        def finish(b):
-            nc.vector.tensor_tensor(out=resid[:, b, :], in0=resid[:, b, :], in1=spread[b][:], op=ADD)
-            nc.sync.dma_start(out=out[b * P : (b + 1) * P, :], in_=resid[:, b, :])
+        def finish(b, parts):
+            for n in range(parts):
+                cols = slice(n * T // parts, (n + 1) * T // parts)
+                nc.vector.tensor_tensor(out=resid[:, b, cols], in0=resid[:, b, cols], in1=window[b][:, cols], op=ADD)
+                nc.sync.dma_start(out=out[b * P : (b + 1) * P, cols], in_=resid[:, b, cols])
 
-        gather(0)
-        first(0, 0)
-        first(0, 1)
-        gather(1)
+        every_block = range(BLOCKS)
+
+        for s in range(PASSES):
+            gather_words(0, s)
+            gather_plane(0, s)
+        first_layer(0)
+        for s in (0, 1, last_pass):
+            gather_words(1, s)
+        for s in range(last_pass):
+            gather_plane(1, s)
+
         hidden(0, 0)
         hidden(0, 1)
-        second(0, 0)
-        second(0, 1)
-        first(1, 0)
-        first(1, 1)
+        gather_words(1, 2)
+        quantise(0, 0)
+        second_layer(0, 0, every_block)
+        leave_psum(0, 0, every_block)
+        gather_plane(1, last_pass)
+        quantise(0, 1)
+        second_layer(0, 1, every_block[:1])
+        leave_psum(0, 1, every_block[:1])
+
+        first_layer(1)
         hidden(1, 0)
         hidden(1, 1)
-        second(1, 0)
-        second(1, 1)
-        for e, j in ((0, 0), (0, 1), (1, 0)):
-            for b in range(BLOCKS):
+        second_layer(0, 1, every_block[1:])
+        leave_psum(0, 1, every_block[1:])
+        quantise(1, 0)
+        second_layer(1, 0, every_block)
+        leave_psum(1, 0, every_block)
+        quantise(1, 1)
+        second_layer(1, 1, every_block)
+        leave_psum(1, 1, every_block[:last_block])
+
+        for e, j in tiles[:-1]:
+            for b in every_block:
                 scatter(e, j, b)
-        scatter(1, 1, 0)
-        scatter(1, 1, 1)
-        finish(0)
-        scatter(1, 1, 2)
-        finish(1)
-        finish(2)
+        for b in every_block[:last_block]:
+            scatter(1, 1, b)
+        finish(0, 1)
+        leave_psum(1, 1, every_block[last_block:])
+        finish(1, 1)
+        scatter(1, 1, last_block)
+        finish(last_block, LAST_PARTS)

from contextlib import ExitStack

import concourse.mybir as mybir
from concourse.masks import make_identity

K, T, E, C, H, N = 2048, 768, 2, 256, 512, 384
FLOPS = 2 * E * C * (2 * K * H + H * N)

F32 = mybir.dt.float32
BF16 = mybir.dt.bfloat16
I32 = mybir.dt.int32
U32 = mybir.dt.uint32
U16 = mybir.dt.uint16
U8 = mybir.dt.uint8
FP8X4 = mybir.dt.float8_e4m3fn_x4
FP4X4 = mybir.dt.float4_e2m1fn_x4
MULT = mybir.AluOpType.mult
ADD = mybir.AluOpType.add
SIGMOID = mybir.ActivationFunctionType.Sigmoid

P = 128
PASSES = K // (4 * P)
HALF = PASSES // 2
TILES = C // P
BLOCKS = N // P
PER_COLUMN = 16
ROWS = 4
BANK = 512
LAST_PARTS = 3

AT_SIGMOID = 0
AT_TURNED = AT_SIGMOID + 4 * H
AT_TABLE = AT_TURNED + 2 * H
AT_WINDOW = AT_TABLE + 4 * T


def tile_moe_res_glu_sigmoid_kernel(
    tc, x_words, x_scales, xr, w1_words, w1_scales, w3_words, w3_scales, w2_words, w2_scales, gate, offs, out
):
    nc = tc.nc
    with ExitStack() as ctx:
        keep = ctx.enter_context(tc.tile_pool(name="keep", bufs=1))
        turns = ctx.enter_context(tc.tile_pool(name="turns", bufs=1))
        psum = ctx.enter_context(tc.psum_pool(name="psum", bufs=1))

        def sbuf(shape, dtype, name, at=None):
            if at is None:
                return keep.tile(shape, dtype, name=name, align_bytes=64)
            return turns.tile(shape, dtype, name=name, align_bytes=64, offset=at)

        tiles = [(e, j) for e in range(E) for j in range(TILES)]
        last_pass, last_block = PASSES - 1, BLOCKS - 1

        offsets = keep.tile([P, E * C // PER_COLUMN], U16, name="offsets")
        x_table = [sbuf([P, T], U32, f"x_table{s}", AT_TABLE if s == last_pass else None) for s in range(PASSES)]
        x_plane = sbuf([P, PASSES, T], U8, "x_plane")
        w_words = {
            (e, m, half): sbuf([P, HALF, 2 * H], U8, f"w_words{e}{m}{half}") for e in range(E) for m in range(2) for half in range(2)
        }
        w_plane = {(e, m): sbuf([P, PASSES, H], U8, f"w_plane{e}{m}") for e in range(E) for m in range(2)}
        w2_sb = sbuf([P, E, 2 * N], U8, "w2_sb")
        w2_plane = sbuf([P, E, N], U8, "w2_plane")
        gate_sb = sbuf([P, E * C], F32, "gate_sb")
        resid = sbuf([P, BLOCKS, T], F32, "resid")
        window = [sbuf([P, T], F32, f"window{b}", AT_WINDOW if b == 0 else None) for b in range(BLOCKS)]
        identity = sbuf([P, P], F32, "identity")
        banks = [psum.tile([P, BANK], F32, name=f"bank{n}") for n in range(2 * len(tiles))]

        slot_words = {
            (e, s): sbuf([P, C], U32, f"slot_words{e}{s}", AT_SIGMOID if (e, s) == (1, 2) else None)
            for e in range(E)
            for s in range(PASSES)
        }
        slot_plane = {(0, s): sbuf([P, C], U8, f"slot_plane0{s}") for s in range(PASSES)}
        for s in range(PASSES):
            slot_plane[1, s] = sbuf([P, C], U8, f"slot_plane1{s}", AT_TURNED if s == last_pass else AT_TABLE + s * C)
        sigmoid = {(e, j): sbuf([P, 2, P, 2], F32, f"sigmoid{e}{j}", AT_SIGMOID if (e, j) == (0, 1) else None) for e, j in tiles}
        h = {(e, j): sbuf([P, 2, P, 2], BF16, f"h{e}{j}") for e, j in tiles}
        h_turned = {(e, j): sbuf([P, 4 * P], BF16, f"h_turned{e}{j}", AT_TURNED if (e, j) == (0, 0) else None) for e, j in tiles}
        h_words = {(e, j): sbuf([P, P], U32, f"h_words{e}{j}") for e, j in tiles}
        h_plane = {(e, j): sbuf([P, P], U8, f"h_plane{e}{j}") for e, j in tiles}
        y = {
            (e, j, b): sbuf([P, P], F32, f"y{e}{j}{b}", AT_WINDOW if (e, j, b) == (1, 1, last_block) else None)
            for e, j in tiles
            for b in range(BLOCKS)
        }

        for plane in (x_plane, w_plane[0, 0], w_plane[0, 1], w2_plane, w_plane[1, 0], w_plane[1, 1]):
            nc.vector.memset(plane[:].rearrange("p a n -> p (a n)").bitcast(I32), 0)
        make_identity(nc, identity[:])
        for b in range(BLOCKS):
            nc.vector.memset(window[b][:], 0.0)

        def load_plane(plane, scales):
            rows = scales.bitcast(I32).rearrange("a (q r) n -> r q a n", r=ROWS)
            for r in range(ROWS):
                nc.sync.dma_start(out=plane[r:P:32, :, :].bitcast(I32), in_=rows[r])

        def load_x(s):
            nc.sync.dma_start(out=x_table[s][:].bitcast(I32), in_=x_words[s].rearrange("p t r -> p (t r)").bitcast(I32))

        def load_w_plane(e, m):
            load_plane(w_plane[e, m], (w1_scales, w3_scales)[m][e])

        def load_w_words(e, m, half):
            words = (w1_words, w3_words)[m][e, half * HALF : (half + 1) * HALF]
            nc.sync.dma_start(out=w_words[e, m, half][:].bitcast(I32), in_=words.bitcast(I32).rearrange("s p n -> p s n"))

        nc.sync.dma_start(offsets[:], offs)
        load_x(0)
        load_plane(x_plane, x_scales)
        load_x(1)
        for m in range(2):
            load_w_plane(0, m)
            load_w_words(0, m, 0)
        load_x(2)
        load_x(3)
        for m in range(2):
            load_w_words(0, m, 1)
        load_w_plane(1, 0)
        load_w_words(1, 0, 0)
        nc.sync.dma_start(out=w2_sb[:].bitcast(I32), in_=w2_words.bitcast(I32).rearrange("e s p n -> p (e s) n"))
        load_plane(w2_plane, w2_scales.rearrange("e s q n -> (e s) q n"))
        load_w_plane(1, 1)
        load_w_words(1, 1, 0)
        nc.sync.dma_start(out=gate_sb[:], in_=gate[0:P, :])
        for m in range(2):
            load_w_words(1, m, 1)
        nc.sync.dma_start(out=resid[:], in_=xr.rearrange("(b p) t -> p b t", p=P))

        def slots(first, count):
            return offsets[:, first // PER_COLUMN : (first + count) // PER_COLUMN]

        def sum_bank(e, j, m):
            return banks[2 * (TILES * e + j) + m]

        def y_bank(e, j, b):
            return sum_bank(1, 0, 1) if (e, j) == (0, 1) and b > 0 else sum_bank(0, j, 1)

        def gather_words(e, s):
            nc.vector.tensor_copy(slot_words[e, s][:], x_table[s][:].indirect(slots(e * C, C)))

        def gather_plane(e, s):
            nc.vector.tensor_copy(slot_plane[e, s][:], x_plane[:, s, :].indirect(slots(e * C, C)))

        def first_pass(e, j, m, s):
            cols = slice(j * P, (j + 1) * P)
            nc.tensor.matmul_mx(
                out=sum_bank(e, j, m)[:],
                lhsT=slot_words[e, s][:, cols].bitcast(FP8X4),
                lhsT_scale=slot_plane[e, s][:, cols],
                rhs=w_words[e, m, s // HALF][:, s % HALF, :].bitcast(FP4X4),
                rhs_scale=w_plane[e, m][:, s, :],
                start=(s == 0),
                stop=(s == last_pass),
            )

        def first_layer(e):
            for m in range(2):
                for s in range(HALF):
                    for j in range(TILES):
                        first_pass(e, j, m, s)
            for j in range(TILES):
                for m in range(2):
                    for s in range(HALF, PASSES):
                        first_pass(e, j, m, s)

        def hidden(e, j):
            order = "c (p u d) -> c u p d"
            nc.scalar.activation(out=sigmoid[e, j][:], in_=sum_bank(e, j, 0)[:].rearrange(order, u=2, d=2), func=SIGMOID)
            nc.vector.tensor_tensor(
                out=h[e, j][:], in0=sum_bank(e, j, 1)[:].rearrange(order, u=2, d=2), in1=sigmoid[e, j][:], op=MULT
            )
            pairs = h[e, j][:].rearrange("c u p d -> c (u p d)").bitcast(F32)
            turned = sum_bank(e, j, 0)
            for u in range(2):
                nc.tensor.transpose(turned[:, u * P : (u + 1) * P], pairs[:, u * P : (u + 1) * P], identity[:])
            nc.scalar.copy(
                out=h_turned[e, j][:].bitcast(F32).rearrange("p (c u) -> p c u", u=2),
                in_=turned[:, 0 : 2 * P].rearrange("p (u c) -> p c u", u=2),
            )

        def quantise(e, j):
            nc.vector.quantize_mx(out=h_words[e, j][:].bitcast(FP8X4), scales=h_plane[e, j][:], in_=h_turned[e, j][:])

        def second_layer(e, j, blocks):
            for b in blocks:
                nc.tensor.matmul_mx(
                    out=y_bank(e, j, b)[:, b * P : (b + 1) * P],
                    lhsT=w2_sb[:, e, 2 * b * P : 2 * (b + 1) * P].bitcast(FP4X4),
                    lhsT_scale=w2_plane[:, e, b * P : (b + 1) * P],
                    rhs=h_words[e, j][:].bitcast(FP8X4),
                    rhs_scale=h_plane[e, j][:],
                    start=True,
                    stop=True,
                )

        def leave_psum(e, j, blocks):
            for b in blocks:
                nc.scalar.copy(out=y[e, j, b][:], in_=y_bank(e, j, b)[:, b * P : (b + 1) * P])

        def scatter(e, j, b):
            first = e * C + j * P
            nc.vector.tensor_tensor(window[b][:].indirect(slots(first, P)), y[e, j, b][:], gate_sb[:, first : first + P], MULT)

        def finish(b, parts):
            for n in range(parts):
                cols = slice(n * T // parts, (n + 1) * T // parts)
                nc.vector.tensor_tensor(out=resid[:, b, cols], in0=resid[:, b, cols], in1=window[b][:, cols], op=ADD)
                nc.sync.dma_start(out=out[b * P : (b + 1) * P, cols], in_=resid[:, b, cols])

        every_block = range(BLOCKS)

        for s in range(PASSES):
            gather_words(0, s)
            gather_plane(0, s)
        first_layer(0)
        for s in (0, 1, last_pass):
            gather_words(1, s)
        for s in range(last_pass):
            gather_plane(1, s)

        hidden(0, 0)
        hidden(0, 1)
        gather_words(1, 2)
        quantise(0, 0)
        second_layer(0, 0, every_block)
        leave_psum(0, 0, every_block)
        gather_plane(1, last_pass)
        quantise(0, 1)
        second_layer(0, 1, every_block[:1])
        leave_psum(0, 1, every_block[:1])

        first_layer(1)
        hidden(1, 0)
        hidden(1, 1)
        second_layer(0, 1, every_block[1:])
        leave_psum(0, 1, every_block[1:])
        quantise(1, 0)
        second_layer(1, 0, every_block)
        leave_psum(1, 0, every_block)
        quantise(1, 1)
        second_layer(1, 1, every_block)
        leave_psum(1, 1, every_block[:last_block])

        for e, j in tiles[:-1]:
            for b in every_block:
                scatter(e, j, b)
        for b in every_block[:last_block]:
            scatter(1, 1, b)
        finish(0, 1)
        leave_psum(1, 1, every_block[last_block:])
        finish(1, 1)
        scatter(1, 1, last_block)
        finish(last_block, LAST_PARTS)
